import numpy as np
import ml_dtypes


def mxq(x, axis, fmt="e4m3"):
    dtype, down = {"e4m3": (ml_dtypes.float8_e4m3fn, 7), "e5m2": (ml_dtypes.float8_e5m2, 14)}[fmt]
    v = np.moveaxis(np.asarray(x, np.float32).astype(ml_dtypes.bfloat16).astype(np.float64), axis, -1)
    blocks = v.reshape(v.shape[:-1] + (-1, 32))
    amax = np.abs(blocks).max(-1, keepdims=True)
    byte = np.maximum(np.where(amax > 0, np.frexp(amax)[1] - 1 + 127, 0) - down, 1)
    scale = np.exp2(byte - 127.0)
    codes = (blocks / scale).astype(np.float32).astype(dtype).astype(np.float64)
    return np.moveaxis((codes * scale).reshape(v.shape), -1, axis)


WIDE = False


def mx_kscale(k):
    if not WIDE:
        return np.ones(k)
    levels = np.array([10, -10, 5, -5, 0])
    if k % 512:
        return np.exp2(np.random.permutation(np.resize(levels, k // 32))).repeat(32)
    a = np.empty((k // 512, 16))
    for p in range(k // 512):
        a[p, :8] = np.random.permutation(np.resize(levels, 8))
        for g in range(8):
            far = levels[np.abs(levels - a[p, g]) >= 10]
            a[p, g + 8] = far[np.random.randint(len(far))]
    return np.exp2(a.ravel()).repeat(32)


def f64(x):
    return np.asarray(x).astype(np.float64)


def striped(idx):
    return np.tile(idx.reshape(-1, 16).T, (8, 1)).astype(np.uint16)


def unstriped(offs):
    return offs[:16].T.reshape(-1).astype(np.int64)


def striped8(idx):
    return np.concatenate([x.reshape(-1, 16).T for x in idx]).astype(np.uint16)


def runs(offs, k):
    lists = np.stack([offs[16 * r : 16 * r + 16].T.reshape(-1) for r in range(8)]).astype(np.int64)
    return lists[np.arange(k) % 512 // 64]


def pack_weight(w):
    k, n = w.shape
    w = f64(np.asarray(w, np.float32).astype(ml_dtypes.bfloat16)).reshape(k // 32, 32, n)
    amax = np.abs(w).max(1)
    byte = np.clip(np.where(amax > 0, np.frexp(amax)[1] - 1 + 127 - 7, 1), 1, 254)
    scaled = (w * np.exp2(127.0 - byte)[:, None, :]).reshape(k, n).astype(np.float32)
    words = np.ascontiguousarray(scaled.reshape(k // 512, 128, 4, n).transpose(0, 1, 3, 2)).astype(ml_dtypes.float8_e4m3fn).view(np.uint8)
    return words, np.ascontiguousarray(byte.astype(np.uint8).reshape(k // 512, 16, n))


def unpack_weight(words, scales):
    g, p, n, _ = words.shape
    vals = np.ascontiguousarray(words).view(ml_dtypes.float8_e4m3fn).astype(np.float64) * np.repeat(np.exp2(scales.astype(np.float64) - 127.0), 8, axis=1)[..., None]
    return vals.transpose(0, 1, 3, 2).reshape(g * 512, n)


def sigmoid(v):
    return 1.0 / (1.0 + np.exp(-np.maximum(v, -700.0)))

def planes(y):
    n, m = y.shape
    v = y.astype(np.float32).astype(ml_dtypes.bfloat16).astype(np.float64).reshape(n // 32, 32, m)
    top = np.abs(v).max(1)
    byte = np.clip(np.where(top > 0, np.frexp(top)[1] - 1 + 127 - 7, 1), 1, 254)
    codes = (v * np.exp2(127.0 - byte)[:, None, :]).reshape(n, m).astype(np.float32).astype(ml_dtypes.float8_e4m3fn).view(np.uint8)
    words = codes.reshape(n // 512, 128, 4, m).transpose(0, 1, 3, 2)
    return np.ascontiguousarray(words), np.ascontiguousarray(byte.astype(np.uint8).reshape(n // 512, 16, m))


K, T, S, N, H, W, G = 512, 2048, 512, 512, 512, 384, 2048


def setup_inputs():
    n = np.random.standard_normal
    s = mx_kscale(K)[:, None]
    u = mx_kscale(S)
    packed_xT = pack_weight(n((K, T)) * s)
    packed_w1 = pack_weight(n((K, H)) / np.sqrt(K) / s)
    packed_w2 = pack_weight(n((H, N)) / np.sqrt(H) / u[:, None])
    packed_dT = pack_weight(n((K, G)) / s)
    return {
        "x_words": packed_xT[0],
        "x_scales": packed_xT[1],
        "w1_words": packed_w1[0],
        "w1_scales": packed_w1[1],
        "gn": (np.random.uniform(0.5, 1.5, (H, 1)) * u[:, None]).astype(np.float32),
        "w2_words": packed_w2[0],
        "w2_scales": packed_w2[1],
        "d_words": packed_dT[0],
        "d_scales": packed_dT[1],
        "offs": striped(np.random.permutation(T)[:S]),
        "n1": striped(np.random.permutation(S)[:W]),
        "n2": striped(np.random.permutation(S)[:W]),
        "two": striped(np.random.permutation(T)[:S]),
        "k1": striped8(np.random.randint(0, G, (8, H))),
        "n3": striped(np.random.permutation(S)),
        "n4": striped(np.random.permutation(S)),
    }


def reference(x_words, x_scales, w1_words, w1_scales, gn, w2_words, w2_scales, d_words, d_scales, offs, n1, n2, two, k1, n3, n4):
    xq = unpack_weight(x_words, x_scales)[:, unstriped(offs)]
    y = unpack_weight(w1_words, w1_scales).T @ xq
    old = y[:, unstriped(n1)]
    pa = y[:, unstriped(n2)]
    ra = old * sigmoid(pa)
    ds = y.copy()
    ds[:, unstriped(n1)] = ra
    z = f64(gn) * ds
    a = unpack_weight(w2_words, w2_scales).T @ mxq(z, 0, "e4m3")
    d_k1 = unpack_weight(d_words, d_scales)[np.arange(K)[:, None], runs(k1, K)]
    x_two = unpack_weight(x_words, x_scales)[:, unstriped(two)]
    b = 0.0625 * (d_k1.T @ x_two)
    out_0 = a * (np.tanh(b[:, unstriped(n3)] - b[:, unstriped(n4)]))
    return (out_0,) + planes(out_0)

@@ -1,0 +1,186 @@
+from contextlib import ExitStack
+
+import concourse.mybir as mybir
+
+K, T, S, N, H, W, G = 512, 2048, 512, 512, 512, 384, 2048
+FLOPS = 3 * 2 * 512 * 512 * 512
+
+F32 = mybir.dt.float32
+BF16 = mybir.dt.bfloat16
+I32 = mybir.dt.int32
+U32 = mybir.dt.uint32
+U16 = mybir.dt.uint16
+U8 = mybir.dt.uint8
+FP8X4 = mybir.dt.float8_e4m3fn_x4
+ACT = mybir.ActivationFunctionType
+ALU = mybir.AluOpType
+
+P = 128
+PACK = 4
+HALF = S // 2
+Y_WINDOW = 768
+SCALAR_SCATTERS = 3
+
+
+def tile_picked_cdjoinjointbkgate_none_po_kernel(
+    tc, x_words, x_scales, w1_words, w1_scales, gn, w2_words, w2_scales, d_words, d_scales,
+    offs, n1, n2, two, k1, n3, n4, out_0, out_1, out_2,
+):
+    nc = tc.nc
+    with ExitStack() as ctx:
+        keep = ctx.enter_context(tc.tile_pool(name="keep", bufs=1))
+        psum = ctx.enter_context(tc.psum_pool(name="psum", bufs=1))
+
+        def tile(shape, dtype, name, tag=None):
+            return keep.tile(shape, dtype, name=name, tag=tag or name, align_bytes=64)
+
+        def load_list(dram, name):
+            t = tile(list(dram.shape), U16, name)
+            nc.sync.dma_start(t[:], dram)
+            return t
+
+        def load_words(queue, dram, name, tag=None):
+            t = tile([P, dram.shape[2]], U32, name, tag)
+            queue.dma_start(t[:].bitcast(I32), dram[0].rearrange("p n b -> p (n b)").bitcast(I32))
+            return t
+
+        def zeroed_bytes(engine, width, name, tag=None):
+            t = tile([P, width], U8, name, tag)
+            engine.memset(t[:].bitcast(I32), 0)
+            return t
+
+        def load_scale_rows(dram, name, tag=None):
+            t = tile([P, dram.shape[2]], U8, name, tag)
+            for q in range(4):
+                rows = dram[0, 4 * q : 4 * q + 4, :].bitcast(I32)
+                nc.sync.dma_start(t[32 * q : 32 * q + 32, :].bitcast(I32), rows.unsqueeze(0).to_broadcast([8, 4, rows.shape[1]]))
+            return t
+
+        def gather(window, offsets, dtype, name):
+            t = tile([P, 16 * offsets.shape[1]], dtype, name)
+            nc.vector.tensor_copy(t[:], window[:].indirect(offsets[:]))
+            return t
+
+        def deal(src, dtype, name):
+            t = tile([P, H], dtype, name)
+            nc.vector.tensor_copy(t[:].rearrange("p (t m) -> p t m", t=PACK), src[:].rearrange("p (m t) -> p t m", t=PACK))
+            return t
+
+        def to_plane(plane, rows):
+            for r in range(4):
+                nc.sync.dma_start(plane[r:P:32, :].bitcast(I32), rows[8 * r : P : 32, :].bitcast(I32))
+
+        def product(out, lhs_words, lhs_scales, t, rhs_words, rhs_scales):
+            cols = slice(P * t, P * (t + 1))
+            nc.tensor.matmul_mx(
+                out, lhsT=lhs_words[:, cols].bitcast(FP8X4), lhsT_scale=lhs_scales[:, cols],
+                rhs=rhs_words.bitcast(FP8X4), rhs_scale=rhs_scales, start=True, stop=True,
+            )
+
+        def interleave(dst, src):
+            nc.vector.tensor_copy(
+                dst[:].rearrange("p (c i t) -> p c t i", i=4, t=PACK), src[:].rearrange("p t (c i) -> p c t i", i=4)
+            )
+
+        offs_t = load_list(offs, "offs_t")
+        xs_table = load_scale_rows(x_scales, "xs_table")
+        xw_table = load_words(nc.sync, x_words, "xw_table")
+        w1w_raw = load_words(nc.sync, w1_words, "w1w_raw")
+        w1s_raw = load_scale_rows(w1_scales, "w1s_raw")
+        two_t = load_list(two, "two_t")
+        k1_t = load_list(k1, "k1_t")
+        dw_table = load_words(nc.sync, d_words, "dw_table")
+        ds_table = zeroed_bytes(nc.vector, G, "ds_table")
+        nc.sync.dma_start(ds_table[0:P:8, :].bitcast(I32), d_scales[0].bitcast(I32))
+        n2_t = load_list(n2, "n2_t")
+        n1_t = load_list(n1, "n1_t")
+        n4_t = load_list(n4, "n4_t")
+        n3_t = load_list(n3, "n3_t")
+        ds_plane = zeroed_bytes(nc.vector, H, "ds_plane")
+        y = [tile([P, Y_WINDOW], F32, f"y{t}") for t in range(PACK)]
+        for t in range(PACK):
+            nc.vector.memset(y[t][:, S:], 0.0)
+
+        xs_idx = gather(xs_table, offs_t, U8, "xs_idx")
+        xw_idx = gather(xw_table, offs_t, U32, "xw_idx")
+        w1w = deal(w1w_raw, U32, "w1w")
+        w1s = deal(w1s_raw, U8, "w1s")
+        y_bank = [psum.tile([P, S], F32, name=f"y_bank{t}", tag=f"low{t}") for t in range(PACK)]
+        for t in range(PACK):
+            product(y_bank[t][:], w1w, w1s, t, xw_idx[:], xs_idx[:])
+
+        xs_two = gather(xs_table, two_t, U8, "xs_two")
+        ds_k1 = gather(ds_table, k1_t, U8, "ds_k1")
+        to_plane(ds_plane, deal(ds_k1, U8, "ds_dealt"))
+        xw_two = gather(xw_table, two_t, U32, "xw_two")
+        w2w_raw = load_words(nc.sync, w2_words, "w2w_raw", "xw_table")
+        gain = tile([P, PACK], F32, "gain", "w1s_raw")
+        nc.sync.dma_start(gain[:], gn.rearrange("(p t) o -> p (t o)", t=PACK))
+        w2s_raw = load_scale_rows(w2_scales, "w2s_raw", "xs_table")
+        dw_k1 = gather(dw_table, k1_t, U32, "dw_k1")
+        dw_dealt = deal(dw_k1, U32, "dw_dealt")
+        b_bank = [psum.tile([P, S], F32, name=f"b_bank{t}", tag=f"high{t}") for t in range(PACK)]
+        for t in range(PACK):
+            product(b_bank[t][:], dw_dealt, ds_plane, t, xw_two[:], xs_two[:])
+
+        sig = [tile([P, W], F32, f"sig{t}") for t in range(PACK)]
+        for t in range(PACK):
+            nc.scalar.copy(y[t][:, :S], y_bank[t][:])
+            nc.scalar.activation(sig[t][:], y[t][:].indirect(n2_t[:]), ACT.Sigmoid)
+        picked = [tile([P, W], F32, f"picked{t}") for t in range(PACK)]
+        for t in range(SCALAR_SCATTERS):
+            nc.vector.tensor_tensor(picked[t][:], y[t][:].indirect(n1_t[:]), sig[t][:], ALU.mult)
+            nc.scalar.activation(y[t][:].indirect(n1_t[:]), picked[t][:], ACT.Copy)
+        for t in range(SCALAR_SCATTERS, PACK):
+            nc.vector.tensor_copy(picked[t][:], y[t][:].indirect(n1_t[:]))
+            nc.vector.tensor_tensor(y[t][:].indirect(n1_t[:]), picked[t][:], sig[t][:], ALU.mult)
+
+        w2w = deal(w2w_raw, U32, "w2w")
+        w2s = deal(w2s_raw, U8, "w2s")
+
+        b = [tile([P, S], F32, f"b{t}") for t in range(PACK)]
+        for t in range(PACK):
+            nc.scalar.copy(b[t][:], b_bank[t][:])
+
+        z_rows = tile([P, PACK, S], BF16, "z_rows")
+        for t in range(PACK):
+            nc.vector.tensor_scalar(z_rows[:, t, :], y[t][:, :S], gain[:, t : t + 1], None, ALU.mult)
+        z_grouped = tile([P, S * PACK], BF16, "z_grouped")
+        interleave(z_grouped, z_rows)
+        z_words = tile([P, S], U32, "z_words")
+        z_scales = tile([P, S], U8, "z_scales")
+        nc.vector.quantize_mx(z_words[:].bitcast(FP8X4), z_scales[:], z_grouped[:])
+
+        a_bank = [psum.tile([P, 2, HALF], F32, name=f"a_bank{i}", tag=f"low{i}") for i in range(PACK)]
+        for h in range(2):
+            cols = slice(HALF * h, HALF * (h + 1))
+            for t in range(PACK):
+                product(a_bank[2 * h + t // 2][:, t % 2, :], w2w, w2s, t, z_words[:, cols], z_scales[:, cols])
+
+        out_rows = out_0.rearrange("(p t) j -> p t j", t=PACK)
+        out_words_hbm = out_1[0].rearrange("p n b -> p (n b)").bitcast(I32)
+        o_words = tile([P, S], U32, "o_words")
+        o_scales = tile([P, S], U8, "o_scales")
+        b4 = [tile([P, PACK, HALF], F32, f"b4_{h}") for h in range(2)]
+        diff = [tile([P, PACK, HALF], F32, f"diff{h}") for h in range(2)]
+        th = [tile([P, PACK, HALF], F32, f"th{h}") for h in range(2)]
+        o = [tile([P, PACK, HALF], F32, f"o{h}") for h in range(2)]
+        o_grouped = [tile([P, PACK * HALF], BF16, f"o_grouped{h}") for h in range(2)]
+        for h in range(2):
+            entries = slice(HALF // 16 * h, HALF // 16 * (h + 1))
+            for t in range(PACK):
+                nc.scalar.activation(b4[h][:, t, :], b[t][:].indirect(n4_t[:, entries]), ACT.Copy)
+                nc.vector.tensor_tensor(diff[h][:, t, :], b[t][:].indirect(n3_t[:, entries]), b4[h][:, t, :], ALU.subtract)
+        for h in range(2):
+            cols = slice(HALF * h, HALF * (h + 1))
+            for u in range(2):
+                pair = slice(2 * u, 2 * u + 2)
+                nc.scalar.activation(th[h][:, pair, :], diff[h][:, pair, :], ACT.Tanh, scale=0.0625)
+                nc.vector.tensor_tensor(o[h][:, pair, :], a_bank[2 * h + u][:], th[h][:, pair, :], ALU.mult)
+            nc.sync.dma_start(out_rows[:, :, cols], o[h][:])
+            interleave(o_grouped[h], o[h])
+            nc.vector.quantize_mx(o_words[:, cols].bitcast(FP8X4), o_scales[:, cols], o_grouped[h][:])
+            nc.sync.dma_start(out_words_hbm[:, cols], o_words[:, cols].bitcast(I32))
+        for q in range(4):
+            queue = nc.sync if q % 2 == 0 else nc.scalar
+            queue.dma_start(out_2[0, 4 * q : 4 * q + 4, :].bitcast(I32), o_scales[32 * q : 32 * q + 4, :].bitcast(I32))

@@ -19,7 +19,7 @@ P = 128
 PACK = 4
 HALF = S // 2
 Y_WINDOW = 768
-SCALAR_SCATTERS = 3
+SCALAR_SCATTERS = 2
 
 
 def tile_picked_cdjoinjointbkgate_none_po_kernel(
@@ -56,8 +56,8 @@ def tile_picked_cdjoinjointbkgate_none_po_kernel(
                 nc.sync.dma_start(t[32 * q : 32 * q + 32, :].bitcast(I32), rows.unsqueeze(0).to_broadcast([8, 4, rows.shape[1]]))
             return t
 
-        def gather(window, offsets, dtype, name):
-            t = tile([P, 16 * offsets.shape[1]], dtype, name)
+        def gather(window, offsets, dtype, name, tag=None):
+            t = tile([P, 16 * offsets.shape[1]], dtype, name, tag)
             nc.vector.tensor_copy(t[:], window[:].indirect(offsets[:]))
             return t
 
@@ -77,17 +77,17 @@ def tile_picked_cdjoinjointbkgate_none_po_kernel(
                 rhs=rhs_words.bitcast(FP8X4), rhs_scale=rhs_scales, start=True, stop=True,
             )
 
-        def interleave(dst, src):
-            nc.vector.tensor_copy(
+        def interleave(copy, dst, src):
+            copy(
                 dst[:].rearrange("p (c i t) -> p c t i", i=4, t=PACK), src[:].rearrange("p t (c i) -> p c t i", i=4)
             )
 
         offs_t = load_list(offs, "offs_t")
         xs_table = load_scale_rows(x_scales, "xs_table")
+        two_t = load_list(two, "two_t")
         xw_table = load_words(nc.sync, x_words, "xw_table")
         w1w_raw = load_words(nc.sync, w1_words, "w1w_raw")
         w1s_raw = load_scale_rows(w1_scales, "w1s_raw")
-        two_t = load_list(two, "two_t")
         k1_t = load_list(k1, "k1_t")
         dw_table = load_words(nc.sync, d_words, "dw_table")
         ds_table = zeroed_bytes(nc.vector, G, "ds_table")
@@ -101,7 +101,11 @@ def tile_picked_cdjoinjointbkgate_none_po_kernel(
         for t in range(PACK):
             nc.vector.memset(y[t][:, S:], 0.0)
 
+        warm = tile([P, 8], F32, "warm")
+        nc.scalar.activation(warm[:], y[0][:, S : S + 8], ACT.Sigmoid)
+
         xs_idx = gather(xs_table, offs_t, U8, "xs_idx")
+        xs_two = gather(xs_table, two_t, U8, "xs_two")
         xw_idx = gather(xw_table, offs_t, U32, "xw_idx")
         w1w = deal(w1w_raw, U32, "w1w")
         w1s = deal(w1s_raw, U8, "w1s")
@@ -109,12 +113,18 @@ def tile_picked_cdjoinjointbkgate_none_po_kernel(
         for t in range(PACK):
             product(y_bank[t][:], w1w, w1s, t, xw_idx[:], xs_idx[:])
 
-        xs_two = gather(xs_table, two_t, U8, "xs_two")
-        ds_k1 = gather(ds_table, k1_t, U8, "ds_k1")
+        sig = [tile([P, W], F32, f"sig{t}") for t in range(PACK)]
+        for t in range(PACK):
+            nc.scalar.copy(y[t][:, :S], y_bank[t][:])
+            nc.scalar.activation(sig[t][:], y[t][:].indirect(n2_t[:]), ACT.Sigmoid)
+        picked = [tile([P, W], F32, f"picked{t}") for t in range(PACK)]
+        nc.scalar.activation(picked[PACK - 1][:], y[PACK - 1][:].indirect(n1_t[:]), ACT.Copy)
+
+        ds_k1 = gather(ds_table, k1_t, U8, "ds_k1", "w1w_raw")
         to_plane(ds_plane, deal(ds_k1, U8, "ds_dealt"))
-        xw_two = gather(xw_table, two_t, U32, "xw_two")
+        xw_two = gather(xw_table, two_t, U32, "xw_two", "w1s_raw")
         w2w_raw = load_words(nc.sync, w2_words, "w2w_raw", "xw_table")
-        gain = tile([P, PACK], F32, "gain", "w1s_raw")
+        gain = tile([P, PACK], F32, "gain", "w1w_raw")
         nc.sync.dma_start(gain[:], gn.rearrange("(p t) o -> p (t o)", t=PACK))
         w2s_raw = load_scale_rows(w2_scales, "w2s_raw", "xs_table")
         dw_k1 = gather(dw_table, k1_t, U32, "dw_k1")
@@ -123,16 +133,12 @@ def tile_picked_cdjoinjointbkgate_none_po_kernel(
         for t in range(PACK):
             product(b_bank[t][:], dw_dealt, ds_plane, t, xw_two[:], xs_two[:])
 
-        sig = [tile([P, W], F32, f"sig{t}") for t in range(PACK)]
-        for t in range(PACK):
-            nc.scalar.copy(y[t][:, :S], y_bank[t][:])
-            nc.scalar.activation(sig[t][:], y[t][:].indirect(n2_t[:]), ACT.Sigmoid)
-        picked = [tile([P, W], F32, f"picked{t}") for t in range(PACK)]
         for t in range(SCALAR_SCATTERS):
             nc.vector.tensor_tensor(picked[t][:], y[t][:].indirect(n1_t[:]), sig[t][:], ALU.mult)
             nc.scalar.activation(y[t][:].indirect(n1_t[:]), picked[t][:], ACT.Copy)
         for t in range(SCALAR_SCATTERS, PACK):
-            nc.vector.tensor_copy(picked[t][:], y[t][:].indirect(n1_t[:]))
+            if t < PACK - 1:
+                nc.vector.tensor_copy(picked[t][:], y[t][:].indirect(n1_t[:]))
             nc.vector.tensor_tensor(y[t][:].indirect(n1_t[:]), picked[t][:], sig[t][:], ALU.mult)
 
         w2w = deal(w2w_raw, U32, "w2w")
@@ -146,7 +152,7 @@ def tile_picked_cdjoinjointbkgate_none_po_kernel(
         for t in range(PACK):
             nc.vector.tensor_scalar(z_rows[:, t, :], y[t][:, :S], gain[:, t : t + 1], None, ALU.mult)
         z_grouped = tile([P, S * PACK], BF16, "z_grouped")
-        interleave(z_grouped, z_rows)
+        interleave(nc.vector.tensor_copy, z_grouped, z_rows)
         z_words = tile([P, S], U32, "z_words")
         z_scales = tile([P, S], U8, "z_scales")
         nc.vector.quantize_mx(z_words[:].bitcast(FP8X4), z_scales[:], z_grouped[:])
@@ -178,7 +184,10 @@ def tile_picked_cdjoinjointbkgate_none_po_kernel(
                 nc.scalar.activation(th[h][:, pair, :], diff[h][:, pair, :], ACT.Tanh, scale=0.0625)
                 nc.vector.tensor_tensor(o[h][:, pair, :], a_bank[2 * h + u][:], th[h][:, pair, :], ALU.mult)
             nc.sync.dma_start(out_rows[:, :, cols], o[h][:])
-            interleave(o_grouped[h], o[h])
+        interleave(nc.scalar.copy, o_grouped[0], o[0])
+        interleave(nc.vector.tensor_copy, o_grouped[1], o[1])
+        for h in range(2):
+            cols = slice(HALF * h, HALF * (h + 1))
             nc.vector.quantize_mx(o_words[:, cols].bitcast(FP8X4), o_scales[:, cols], o_grouped[h][:])
             nc.sync.dma_start(out_words_hbm[:, cols], o_words[:, cols].bitcast(I32))
         for q in range(4):

from contextlib import ExitStack

import concourse.mybir as mybir

K, T, S, N, H, W, G = 512, 2048, 512, 512, 512, 384, 2048
FLOPS = 3 * 2 * 512 * 512 * 512

F32 = mybir.dt.float32
BF16 = mybir.dt.bfloat16
I32 = mybir.dt.int32
U32 = mybir.dt.uint32
U16 = mybir.dt.uint16
U8 = mybir.dt.uint8
FP8X4 = mybir.dt.float8_e4m3fn_x4
ACT = mybir.ActivationFunctionType
ALU = mybir.AluOpType

P = 128
PACK = 4
HALF = S // 2
Y_WINDOW = 768
SCALAR_SCATTERS = 2


def tile_picked_cdjoinjointbkgate_none_po_kernel(
    tc, x_words, x_scales, w1_words, w1_scales, gn, w2_words, w2_scales, d_words, d_scales,
    offs, n1, n2, two, k1, n3, n4, out_0, out_1, out_2,
):
    nc = tc.nc
    with ExitStack() as ctx:
        keep = ctx.enter_context(tc.tile_pool(name="keep", bufs=1))
        psum = ctx.enter_context(tc.psum_pool(name="psum", bufs=1))

        def tile(shape, dtype, name, tag=None):
            return keep.tile(shape, dtype, name=name, tag=tag or name, align_bytes=64)

        def load_list(dram, name):
            t = tile(list(dram.shape), U16, name)
            nc.sync.dma_start(t[:], dram)
            return t

        def load_words(queue, dram, name, tag=None):
            t = tile([P, dram.shape[2]], U32, name, tag)
            queue.dma_start(t[:].bitcast(I32), dram[0].rearrange("p n b -> p (n b)").bitcast(I32))
            return t

        def zeroed_bytes(engine, width, name, tag=None):
            t = tile([P, width], U8, name, tag)
            engine.memset(t[:].bitcast(I32), 0)
            return t

        def load_scale_rows(dram, name, tag=None):
            t = tile([P, dram.shape[2]], U8, name, tag)
            for q in range(4):
                rows = dram[0, 4 * q : 4 * q + 4, :].bitcast(I32)
                nc.sync.dma_start(t[32 * q : 32 * q + 32, :].bitcast(I32), rows.unsqueeze(0).to_broadcast([8, 4, rows.shape[1]]))
            return t

        def gather(window, offsets, dtype, name, tag=None):
            t = tile([P, 16 * offsets.shape[1]], dtype, name, tag)
            nc.vector.tensor_copy(t[:], window[:].indirect(offsets[:]))
            return t

        def deal(src, dtype, name):
            t = tile([P, H], dtype, name)
            nc.vector.tensor_copy(t[:].rearrange("p (t m) -> p t m", t=PACK), src[:].rearrange("p (m t) -> p t m", t=PACK))
            return t

        def to_plane(plane, rows):
            for r in range(4):
                nc.sync.dma_start(plane[r:P:32, :].bitcast(I32), rows[8 * r : P : 32, :].bitcast(I32))

        def product(out, lhs_words, lhs_scales, t, rhs_words, rhs_scales):
            cols = slice(P * t, P * (t + 1))
            nc.tensor.matmul_mx(
                out, lhsT=lhs_words[:, cols].bitcast(FP8X4), lhsT_scale=lhs_scales[:, cols],
                rhs=rhs_words.bitcast(FP8X4), rhs_scale=rhs_scales, start=True, stop=True,
            )

        def interleave(copy, dst, src):
            copy(
                dst[:].rearrange("p (c i t) -> p c t i", i=4, t=PACK), src[:].rearrange("p t (c i) -> p c t i", i=4)
            )

        offs_t = load_list(offs, "offs_t")
        xs_table = load_scale_rows(x_scales, "xs_table")
        two_t = load_list(two, "two_t")
        xw_table = load_words(nc.sync, x_words, "xw_table")
        w1w_raw = load_words(nc.sync, w1_words, "w1w_raw")
        w1s_raw = load_scale_rows(w1_scales, "w1s_raw")
        k1_t = load_list(k1, "k1_t")
        dw_table = load_words(nc.sync, d_words, "dw_table")
        ds_table = zeroed_bytes(nc.vector, G, "ds_table")
        nc.sync.dma_start(ds_table[0:P:8, :].bitcast(I32), d_scales[0].bitcast(I32))
        n2_t = load_list(n2, "n2_t")
        n1_t = load_list(n1, "n1_t")
        n4_t = load_list(n4, "n4_t")
        n3_t = load_list(n3, "n3_t")
        ds_plane = zeroed_bytes(nc.vector, H, "ds_plane")
        y = [tile([P, Y_WINDOW], F32, f"y{t}") for t in range(PACK)]
        for t in range(PACK):
            nc.vector.memset(y[t][:, S:], 0.0)

        warm = tile([P, 8], F32, "warm")
        nc.scalar.activation(warm[:], y[0][:, S : S + 8], ACT.Sigmoid)

        xs_idx = gather(xs_table, offs_t, U8, "xs_idx")
        xs_two = gather(xs_table, two_t, U8, "xs_two")
        xw_idx = gather(xw_table, offs_t, U32, "xw_idx")
        w1w = deal(w1w_raw, U32, "w1w")
        w1s = deal(w1s_raw, U8, "w1s")
        y_bank = [psum.tile([P, S], F32, name=f"y_bank{t}", tag=f"low{t}") for t in range(PACK)]
        for t in range(PACK):
            product(y_bank[t][:], w1w, w1s, t, xw_idx[:], xs_idx[:])

        sig = [tile([P, W], F32, f"sig{t}") for t in range(PACK)]
        for t in range(PACK):
            nc.scalar.copy(y[t][:, :S], y_bank[t][:])
            nc.scalar.activation(sig[t][:], y[t][:].indirect(n2_t[:]), ACT.Sigmoid)
        picked = [tile([P, W], F32, f"picked{t}") for t in range(PACK)]
        nc.scalar.activation(picked[PACK - 1][:], y[PACK - 1][:].indirect(n1_t[:]), ACT.Copy)

        ds_k1 = gather(ds_table, k1_t, U8, "ds_k1", "w1w_raw")
        to_plane(ds_plane, deal(ds_k1, U8, "ds_dealt"))
        xw_two = gather(xw_table, two_t, U32, "xw_two", "w1s_raw")
        w2w_raw = load_words(nc.sync, w2_words, "w2w_raw", "xw_table")
        gain = tile([P, PACK], F32, "gain", "w1w_raw")
        nc.sync.dma_start(gain[:], gn.rearrange("(p t) o -> p (t o)", t=PACK))
        w2s_raw = load_scale_rows(w2_scales, "w2s_raw", "xs_table")
        dw_k1 = gather(dw_table, k1_t, U32, "dw_k1")
        dw_dealt = deal(dw_k1, U32, "dw_dealt")
        b_bank = [psum.tile([P, S], F32, name=f"b_bank{t}", tag=f"high{t}") for t in range(PACK)]
        for t in range(PACK):
            product(b_bank[t][:], dw_dealt, ds_plane, t, xw_two[:], xs_two[:])

        for t in range(SCALAR_SCATTERS):
            nc.vector.tensor_tensor(picked[t][:], y[t][:].indirect(n1_t[:]), sig[t][:], ALU.mult)
            nc.scalar.activation(y[t][:].indirect(n1_t[:]), picked[t][:], ACT.Copy)
        for t in range(SCALAR_SCATTERS, PACK):
            if t < PACK - 1:
                nc.vector.tensor_copy(picked[t][:], y[t][:].indirect(n1_t[:]))
            nc.vector.tensor_tensor(y[t][:].indirect(n1_t[:]), picked[t][:], sig[t][:], ALU.mult)

        w2w = deal(w2w_raw, U32, "w2w")
        w2s = deal(w2s_raw, U8, "w2s")

        b = [tile([P, S], F32, f"b{t}") for t in range(PACK)]
        for t in range(PACK):
            nc.scalar.copy(b[t][:], b_bank[t][:])

        z_rows = tile([P, PACK, S], BF16, "z_rows")
        for t in range(PACK):
            nc.vector.tensor_scalar(z_rows[:, t, :], y[t][:, :S], gain[:, t : t + 1], None, ALU.mult)
        z_grouped = tile([P, S * PACK], BF16, "z_grouped")
        interleave(nc.vector.tensor_copy, z_grouped, z_rows)
        z_words = tile([P, S], U32, "z_words")
        z_scales = tile([P, S], U8, "z_scales")
        nc.vector.quantize_mx(z_words[:].bitcast(FP8X4), z_scales[:], z_grouped[:])

        a_bank = [psum.tile([P, 2, HALF], F32, name=f"a_bank{i}", tag=f"low{i}") for i in range(PACK)]
        for h in range(2):
            cols = slice(HALF * h, HALF * (h + 1))
            for t in range(PACK):
                product(a_bank[2 * h + t // 2][:, t % 2, :], w2w, w2s, t, z_words[:, cols], z_scales[:, cols])

        out_rows = out_0.rearrange("(p t) j -> p t j", t=PACK)
        out_words_hbm = out_1[0].rearrange("p n b -> p (n b)").bitcast(I32)
        o_words = tile([P, S], U32, "o_words")
        o_scales = tile([P, S], U8, "o_scales")
        b4 = [tile([P, PACK, HALF], F32, f"b4_{h}") for h in range(2)]
        diff = [tile([P, PACK, HALF], F32, f"diff{h}") for h in range(2)]
        th = [tile([P, PACK, HALF], F32, f"th{h}") for h in range(2)]
        o = [tile([P, PACK, HALF], F32, f"o{h}") for h in range(2)]
        o_grouped = [tile([P, PACK * HALF], BF16, f"o_grouped{h}") for h in range(2)]
        for h in range(2):
            entries = slice(HALF // 16 * h, HALF // 16 * (h + 1))
            for t in range(PACK):
                nc.scalar.activation(b4[h][:, t, :], b[t][:].indirect(n4_t[:, entries]), ACT.Copy)
                nc.vector.tensor_tensor(diff[h][:, t, :], b[t][:].indirect(n3_t[:, entries]), b4[h][:, t, :], ALU.subtract)
        for h in range(2):
            cols = slice(HALF * h, HALF * (h + 1))
            for u in range(2):
                pair = slice(2 * u, 2 * u + 2)
                nc.scalar.activation(th[h][:, pair, :], diff[h][:, pair, :], ACT.Tanh, scale=0.0625)
                nc.vector.tensor_tensor(o[h][:, pair, :], a_bank[2 * h + u][:], th[h][:, pair, :], ALU.mult)
            nc.sync.dma_start(out_rows[:, :, cols], o[h][:])
        interleave(nc.scalar.copy, o_grouped[0], o[0])
        interleave(nc.vector.tensor_copy, o_grouped[1], o[1])
        for h in range(2):
            cols = slice(HALF * h, HALF * (h + 1))
            nc.vector.quantize_mx(o_words[:, cols].bitcast(FP8X4), o_scales[:, cols], o_grouped[h][:])
            nc.sync.dma_start(out_words_hbm[:, cols], o_words[:, cols].bitcast(I32))
        for q in range(4):
            queue = nc.sync if q % 2 == 0 else nc.scalar
            queue.dma_start(out_2[0, 4 * q : 4 * q + 4, :].bitcast(I32), o_scales[32 * q : 32 * q + 4, :].bitcast(I32))
